import numpy as np
import ml_dtypes


def mxq(x, axis, fmt="e4m3"):
    dtype, down = {"e4m3": (ml_dtypes.float8_e4m3fn, 7), "e5m2": (ml_dtypes.float8_e5m2, 14)}[fmt]
    v = np.moveaxis(np.asarray(x, np.float32).astype(ml_dtypes.bfloat16).astype(np.float64), axis, -1)
    blocks = v.reshape(v.shape[:-1] + (-1, 32))
    amax = np.abs(blocks).max(-1, keepdims=True)
    byte = np.maximum(np.where(amax > 0, np.frexp(amax)[1] - 1 + 127, 0) - down, 1)
    scale = np.exp2(byte - 127.0)
    codes = (blocks / scale).astype(np.float32).astype(dtype).astype(np.float64)
    return np.moveaxis((codes * scale).reshape(v.shape), -1, axis)


WIDE = False


def mx_kscale(k):
    if not WIDE:
        return np.ones(k)
    levels = np.array([10, -10, 5, -5, 0])
    if k % 512:
        return np.exp2(np.random.permutation(np.resize(levels, k // 32))).repeat(32)
    a = np.empty((k // 512, 16))
    for p in range(k // 512):
        a[p, :8] = np.random.permutation(np.resize(levels, 8))
        for g in range(8):
            far = levels[np.abs(levels - a[p, g]) >= 10]
            a[p, g + 8] = far[np.random.randint(len(far))]
    return np.exp2(a.ravel()).repeat(32)


def f64(x):
    return np.asarray(x).astype(np.float64)


def striped(idx):
    return np.tile(idx.reshape(-1, 16).T, (8, 1)).astype(np.uint16)


def unstriped(offs):
    return offs[:16].T.reshape(-1).astype(np.int64)


def striped8(idx):
    return np.concatenate([x.reshape(-1, 16).T for x in idx]).astype(np.uint16)


def runs(offs, k):
    lists = np.stack([offs[16 * r : 16 * r + 16].T.reshape(-1) for r in range(8)]).astype(np.int64)
    return lists[np.arange(k) % 512 // 64]


def pack_weight(w):
    k, n = w.shape
    w = f64(np.asarray(w, np.float32).astype(ml_dtypes.bfloat16)).reshape(k // 32, 32, n)
    amax = np.abs(w).max(1)
    byte = np.clip(np.where(amax > 0, np.frexp(amax)[1] - 1 + 127 - 7, 1), 1, 254)
    scaled = (w * np.exp2(127.0 - byte)[:, None, :]).reshape(k, n).astype(np.float32)
    words = np.ascontiguousarray(scaled.reshape(k // 512, 128, 4, n).transpose(0, 1, 3, 2)).astype(ml_dtypes.float8_e4m3fn).view(np.uint8)
    return words, np.ascontiguousarray(byte.astype(np.uint8).reshape(k // 512, 16, n))


def unpack_weight(words, scales):
    g, p, n, _ = words.shape
    vals = np.ascontiguousarray(words).view(ml_dtypes.float8_e4m3fn).astype(np.float64) * np.repeat(np.exp2(scales.astype(np.float64) - 127.0), 8, axis=1)[..., None]
    return vals.transpose(0, 1, 3, 2).reshape(g * 512, n)


E2M1 = np.array([0.0, 0.5, 1.0, 1.5, 2.0, 3.0, 4.0, 6.0, -0.0, -0.5, -1.0, -1.5, -2.0, -3.0, -4.0, -6.0])


def pack_fp4(w):
    k, n = w.shape
    w = f64(np.asarray(w, np.float32).astype(ml_dtypes.bfloat16)).reshape(k // 32, 32, n)
    amax = np.abs(w).max(1)
    mant, ex = np.frexp(amax / 6.0)
    byte = np.clip(np.where(amax > 0, np.where(mant > 0.5, ex, ex - 1) + 127, 1), 1, 254)
    scaled = (w * np.exp2(127.0 - byte)[:, None, :]).reshape(k, n).astype(np.float32)
    c = np.ascontiguousarray(scaled.reshape(k // 512, 128, 4, n).transpose(0, 1, 3, 2)).astype(ml_dtypes.float4_e2m1fn).view(np.uint8) & 0xF
    words = (c[..., 0::2] | (c[..., 1::2] << 4)).reshape(k // 512, 128, 2 * n)
    return np.ascontiguousarray(words), np.ascontiguousarray(byte.astype(np.uint8).reshape(k // 512, 16, n))


def unpack_fp4(words, scales):
    g, _, n = scales.shape
    words = np.ascontiguousarray(words).reshape(g, 128, n, 2)
    nib = np.empty((g, 128, n, 4), np.uint8)
    nib[..., 0::2] = words & 0xF
    nib[..., 1::2] = words >> 4
    vals = E2M1[nib] * np.repeat(np.exp2(scales.astype(np.float64) - 127.0), 8, axis=1)[..., None]
    return vals.transpose(0, 1, 3, 2).reshape(g * 512, n)


def planes(y):
    n, m = y.shape
    v = y.astype(np.float32).astype(ml_dtypes.bfloat16).astype(np.float64).reshape(n // 32, 32, m)
    top = np.abs(v).max(1)
    byte = np.clip(np.where(top > 0, np.frexp(top)[1] - 1 + 127 - 7, 1), 1, 254)
    codes = (v * np.exp2(127.0 - byte)[:, None, :]).reshape(n, m).astype(np.float32).astype(ml_dtypes.float8_e4m3fn).view(np.uint8)
    words = codes.reshape(n // 512, 128, 4, m).transpose(0, 1, 3, 2)
    return np.ascontiguousarray(words), np.ascontiguousarray(byte.astype(np.uint8).reshape(n // 512, 16, m))


K, T, S, V, H, U = 512, 2048, 512, 512, 512, 1024


def setup_inputs():
    n = np.random.standard_normal
    s = mx_kscale(K)[:, None]
    u = mx_kscale(S)
    packed_xT = pack_weight(n((K, T)) * s)
    packed_w1 = pack_fp4(n((K, H)) / np.sqrt(K) / s)
    packed_w2 = pack_fp4(n((K, H)) / np.sqrt(K) / s)
    return {
        "x_words": packed_xT[0],
        "x_scales": packed_xT[1],
        "w1_words": packed_w1[0],
        "w1_scales": packed_w1[1],
        "w2_words": packed_w2[0],
        "w2_scales": packed_w2[1],
        "mem": n((H, U)).astype(np.float32),
        "ga": (np.random.uniform(0.5, 1.5, (H, 1)) * u[:, None]).astype(np.float32),
        "gb": (np.random.uniform(0.5, 1.5, (H, 1)) / u[:, None]).astype(np.float32),
        "offs": striped(np.random.permutation(T)[:S]),
        "two": striped(np.random.permutation(T)[:V]),
        "slot": striped8(np.stack([np.random.permutation(U)[:S] for _ in range(8)])),
        "nq": striped8(np.stack([np.random.permutation(V) for _ in range(8)])),
    }


def reference(x_words, x_scales, w1_words, w1_scales, w2_words, w2_scales, mem, ga, gb, offs, two, slot, nq):
    xq = unpack_weight(x_words, x_scales)[:, unstriped(offs)]
    a = unpack_fp4(w1_words, w1_scales).T @ xq
    pg = f64(mem).copy()
    pg[np.arange(H)[:, None], runs(slot, H)] = a
    z = f64(ga) * pg
    x_two = unpack_weight(x_words, x_scales)[:, unstriped(two)]
    b = unpack_fp4(w2_words, w2_scales).T @ x_two
    z2 = f64(gb) * (np.maximum(b, b[np.arange(H)[:, None], runs(nq, H)]))
    s = 0.0625 * ((mxq(z, 0, "e4m3").T @ mxq(z2, 0, "e4m3")))
    out_0 = np.tanh(s)
    return (out_0,) + planes(out_0)

@@ -1,0 +1,212 @@
+from contextlib import ExitStack
+
+import concourse.mybir as mybir
+
+F32 = mybir.dt.float32
+BF16 = mybir.dt.bfloat16
+I32 = mybir.dt.int32
+U32 = mybir.dt.uint32
+U16 = mybir.dt.uint16
+U8 = mybir.dt.uint8
+FP8X4 = mybir.dt.float8_e4m3fn_x4
+FP4X4 = mybir.dt.float4_e2m1fn_x4
+ALU = mybir.AluOpType
+ACT = mybir.ActivationFunctionType
+
+K, T, S, V, H, U = 512, 2048, 512, 512, 512, 1024
+P = 128
+PACK = 4
+GROUPS = U // 512
+HALVES = 2
+VH = V // HALVES
+
+FLOPS = 2 * K * H * S + 2 * K * H * V + 2 * H * U * V
+
+
+def tile_picked_keypage_none_po_kernel(tc, x_words, x_scales, w1_words, w1_scales, w2_words, w2_scales, mem, ga, gb, offs, two, slot, nq, out_0, out_1, out_2):
+    nc = tc.nc
+    with ExitStack() as ctx:
+        sb = ctx.enter_context(tc.tile_pool(name="sb", bufs=1))
+        ps = ctx.enter_context(tc.psum_pool(name="ps", bufs=1))
+
+        def tile(name, shape, dtype, tag=None):
+            return sb.tile(shape, dtype, name=name, tag=tag or name, align_bytes=64)
+
+        offs_t = sb.tile([P, S // 16], U16, name="offs_t")
+        two_t = sb.tile([P, V // 16], U16, name="two_t")
+        slot_t = sb.tile([P, S // 16], U16, name="slot_t")
+        nq_t = sb.tile([P, V // 16], U16, name="nq_t")
+
+        xw = tile("xw", [P, T], I32)
+        xs = tile("xs", [P, T], U8)
+        ww = [tile("ww%d" % i, [P, 2 * H], U8) for i in range(2)]
+        ws = [tile("ws%d" % i, [P, H], U8) for i in range(2)]
+        page = [tile("page%d" % t, [P, U], F32) for t in range(PACK)]
+        ga_t = tile("ga_t", [P, PACK], F32)
+        gb_t = tile("gb_t", [P, PACK], F32)
+
+        def load_scales(queue, dst, src):
+            for q in range(4):
+                queue.dma_start(out=dst[32 * q : 32 * q + 4, :].bitcast(I32), in_=src[0, 4 * q : 4 * q + 4, :].bitcast(I32))
+
+        nc.vector.memset(xs[:].bitcast(I32), 0)
+        nc.vector.memset(ws[0][:].bitcast(I32), 0)
+        nc.vector.memset(ws[1][:].bitcast(I32), 0)
+        warm = tile("warm", [P, 2], F32)
+        nc.gpsimd.memset(warm[:, 0:1], 0.0)
+        nc.scalar.activation(out=warm[:, 1:2], in_=warm[:, 0:1], func=ACT.Tanh)
+
+        nc.sync.dma_start(offs_t[:], offs)
+        nc.sync.dma_start(two_t[:], two)
+        load_scales(nc.sync, xs, x_scales)
+        nc.sync.dma_start(out=ww[0][:].bitcast(I32), in_=w1_words[0].bitcast(I32))
+        nc.sync.dma_start(out=xw[:], in_=x_words[0].rearrange("p n t -> p (n t)").bitcast(I32))
+        load_scales(nc.sync, ws[0], w1_scales)
+        nc.sync.dma_start(slot_t[:], slot)
+        mem_rows = mem.rearrange("(p t) u -> t p u", t=PACK)
+        nc.sync.dma_start(out=ww[1][:].bitcast(I32), in_=w2_words[0].bitcast(I32))
+        nc.sync.dma_start(out=page[0][:], in_=mem_rows[0])
+        load_scales(nc.sync, ws[1], w2_scales)
+        for t in range(1, PACK):
+            nc.sync.dma_start(out=page[t][:], in_=mem_rows[t])
+        nc.sync.dma_start(nq_t[:], nq)
+        nc.gpsimd.dma_start(out=gb_t[:], in_=gb.rearrange("(p t) o -> p (t o)", t=PACK))
+        nc.gpsimd.dma_start(out=ga_t[:], in_=ga.rearrange("(p t) o -> p (t o)", t=PACK))
+
+        twice = tile("twice", [P, PACK], F32)
+        sign = tile("sign", [P, PACK], F32)
+        gb_abs = tile("gb_abs", [P, PACK], F32)
+        ga_signed = tile("ga_signed", [P, PACK], F32)
+        nc.gpsimd.tensor_scalar(out=twice[:], in0=gb_t[:], scalar1=0.0, scalar2=2.0, op0=ALU.is_ge, op1=ALU.mult)
+        nc.gpsimd.tensor_scalar(out=sign[:], in0=twice[:], scalar1=1.0, scalar2=-1.0, op0=ALU.mult, op1=ALU.add)
+        nc.gpsimd.tensor_tensor(out=gb_abs[:], in0=gb_t[:], in1=sign[:], op=ALU.mult)
+        nc.gpsimd.tensor_tensor(out=ga_signed[:], in0=ga_t[:], in1=sign[:], op=ALU.mult)
+
+        lists = [offs_t, two_t]
+        pw = [tile("pw%d" % i, [P, S], U32) for i in range(2)]
+        pscale = [tile("pscale%d" % i, [P, S], U8) for i in range(2)]
+        dw = [tile("dw%d" % i, [P, 2 * H], U8) for i in range(2)]
+        ds = [tile("ds%d" % i, [P, H], U8) for i in range(2)]
+
+        def gather_scales(i):
+            nc.vector.tensor_copy(pscale[i][:], xs[:].indirect(lists[i][:]))
+
+        def gather_words(i):
+            nc.vector.tensor_copy(pw[i][:], xw[:].bitcast(U32).indirect(lists[i][:]))
+
+        def deal_words(i):
+            nc.vector.tensor_copy(out=dw[i][:].rearrange("p (t m b) -> p t m b", t=PACK, b=2), in_=ww[i][:].rearrange("p (m t b) -> p t m b", t=PACK, b=2))
+
+        def deal_scales(i):
+            nc.vector.tensor_copy(out=ds[i][:].rearrange("p (t m) -> p t m", t=PACK), in_=ws[i][:].rearrange("p (m t) -> p t m", t=PACK))
+
+        def project(i, t):
+            bank = ps.tile([P, S], F32, name="proj%d_%d" % (i, t), tag="bank%d" % (PACK * i + t))
+            nc.tensor.matmul_mx(
+                out=bank[:],
+                lhsT=dw[i][:, 2 * P * t : 2 * P * (t + 1)].bitcast(FP4X4),
+                lhsT_scale=ds[i][:, P * t : P * (t + 1)],
+                rhs=pw[i][:].bitcast(FP8X4),
+                rhs_scale=pscale[i][:],
+                start=True,
+                stop=True,
+            )
+            return bank
+
+        gather_scales(0)
+        gather_scales(1)
+        deal_words(0)
+        gather_words(0)
+        deal_scales(0)
+        gather_words(1)
+        deal_words(1)
+        deal_scales(1)
+
+        a_sb = [tile("a_sb%d" % t, [P, S], F32) for t in range(PACK)]
+        for t in range(PACK):
+            bank = project(0, t)
+            nc.scalar.copy(out=a_sb[t][:], in_=bank[:])
+        yw = [tile("yw%d" % t, [P, V], F32) for t in range(PACK)]
+        y_all = tile("y_all", [P, PACK, V], F32)
+        for t in range(PACK):
+            bank = project(1, t)
+            nc.scalar.activation(out=yw[t][:], in_=bank[:], func=ACT.Copy, scale=gb_abs[:, t : t + 1])
+            nc.sync.dma_start(out=y_all[:, t, :], in_=yw[t][:])
+
+        zb = [tile("zb%d" % g, [P, PACK * 512], BF16, tag="shared%d" % g) for g in range(GROUPS)]
+        for t in range(PACK):
+            nc.vector.tensor_copy(page[t][:].indirect(slot_t[:]), a_sb[t][:])
+            for g in range(GROUPS):
+                nc.scalar.activation(
+                    out=zb[g][:].rearrange("p (j m k) -> p j m k", j=PACK, k=PACK)[:, :, :, t],
+                    in_=page[t][:, 512 * g : 512 * (g + 1)].rearrange("p (m j) -> p j m", j=PACK),
+                    func=ACT.Copy,
+                    scale=ga_signed[:, t : t + 1],
+                )
+
+        zc = [tile("zc%d" % g, [P, 512], U32) for g in range(GROUPS)]
+        zs = [tile("zs%d" % g, [P, 512], U8) for g in range(GROUPS)]
+        qc = [tile("qc%d" % h, [P, VH], U32) for h in range(HALVES)]
+        qs = [tile("qs%d" % h, [P, VH], U8) for h in range(HALVES)]
+        oc = [tile("oc%d" % g, [P, V], U32) for g in range(GROUPS)]
+        osc = tile("osc", [P, GROUPS, V], U8)
+
+        def queries(h):
+            got = tile("got%d" % h, [P, PACK, VH], F32, tag="got0" if h == 0 else "shared1")
+            for t in range(PACK):
+                nc.vector.tensor_copy(got[:, t, :], yw[t][:].indirect(nq_t[:, h * VH // 16 : (h + 1) * VH // 16]))
+            qb = tile("qb%d" % h, [P, PACK * VH], BF16)
+            nc.vector.tensor_tensor(
+                out=qb[:].rearrange("p (c i t) -> p c t i", i=2, t=PACK),
+                in0=got[:].rearrange("p t (c i) -> p c t i", i=2),
+                in1=y_all[:, :, h * VH : (h + 1) * VH].rearrange("p t (c i) -> p c t i", i=2),
+                op=ALU.max,
+            )
+            nc.vector.quantize_mx(out=qc[h][:].bitcast(FP8X4), scales=qs[h][:], in_=qb[:])
+
+        def scores(h, g):
+            y = tile("y%d_%d" % (h, g), [P, PACK, VH], F32)
+            for pair in range(2):
+                bank = ps.tile([P, 2, VH], F32, name="score%d_%d_%d" % (h, g, pair), tag="bank%d" % (PACK * h + 2 * g + pair))
+                for e in range(2):
+                    j = 2 * pair + e
+                    nc.tensor.matmul_mx(
+                        out=bank[:, e, :],
+                        lhsT=zc[g][:, P * j : P * (j + 1)].bitcast(FP8X4),
+                        lhsT_scale=zs[g][:, P * j : P * (j + 1)],
+                        rhs=qc[h][:].bitcast(FP8X4),
+                        rhs_scale=qs[h][:],
+                        start=True,
+                        stop=True,
+                    )
+                nc.scalar.activation(out=y[:, 2 * pair : 2 * pair + 2, :], in_=bank[:], func=ACT.Tanh, scale=0.0625)
+            cols = slice(h * VH, (h + 1) * VH)
+            nc.sync.dma_start(out=out_0[512 * g : 512 * (g + 1), cols].rearrange("(p j) v -> p j v", j=PACK), in_=y[:])
+            return y
+
+        def planes(h, g, y):
+            yb = tile("yb%d_%d" % (h, g), [P, PACK * VH], BF16)
+            nc.vector.tensor_copy(
+                out=yb[:].rearrange("p (c i j) -> p c j i", i=2, j=PACK),
+                in_=y[:].rearrange("p j (c i) -> p c j i", i=2),
+            )
+            cols = slice(h * VH, (h + 1) * VH)
+            nc.vector.quantize_mx(out=oc[g][:, cols].bitcast(FP8X4), scales=osc[:, g, cols], in_=yb[:])
+            nc.sync.dma_start(out=out_1[g].rearrange("p v t -> p (v t)").bitcast(I32)[:, cols], in_=oc[g][:, cols].bitcast(I32))
+
+        queries(0)
+        for g in range(GROUPS):
+            nc.vector.quantize_mx(out=zc[g][:].bitcast(FP8X4), scales=zs[g][:], in_=zb[g][:])
+        first = [scores(0, g) for g in range(GROUPS)]
+        queries(1)
+        second = [scores(1, g) for g in range(GROUPS)]
+        for g in range(GROUPS):
+            planes(0, g, first[g])
+        for g in range(GROUPS):
+            planes(1, g, second[g])
+        for q in range(4):
+            queue = nc.sync if q % 2 == 0 else nc.scalar
+            queue.dma_start(
+                out=out_2[:, 4 * q : 4 * q + 4, :].rearrange("g r v -> r g v").bitcast(I32),
+                in_=osc[32 * q : 32 * q + 4, :, :].bitcast(I32),
+            )

@@ -41,7 +41,6 @@ def tile_picked_keypage_none_po_kernel(tc, x_words, x_scales, w1_words, w1_scale
         xs = tile("xs", [P, T], U8)
         ww = [tile("ww%d" % i, [P, 2 * H], U8) for i in range(2)]
         ws = [tile("ws%d" % i, [P, H], U8) for i in range(2)]
-        page = [tile("page%d" % t, [P, U], F32) for t in range(PACK)]
         ga_t = tile("ga_t", [P, PACK], F32)
         gb_t = tile("gb_t", [P, PACK], F32)
 
@@ -49,12 +48,9 @@ def tile_picked_keypage_none_po_kernel(tc, x_words, x_scales, w1_words, w1_scale
             for q in range(4):
                 queue.dma_start(out=dst[32 * q : 32 * q + 4, :].bitcast(I32), in_=src[0, 4 * q : 4 * q + 4, :].bitcast(I32))
 
-        nc.vector.memset(xs[:].bitcast(I32), 0)
+        nc.gpsimd.memset(xs[:].bitcast(I32), 0)
         nc.vector.memset(ws[0][:].bitcast(I32), 0)
         nc.vector.memset(ws[1][:].bitcast(I32), 0)
-        warm = tile("warm", [P, 2], F32)
-        nc.gpsimd.memset(warm[:, 0:1], 0.0)
-        nc.scalar.activation(out=warm[:, 1:2], in_=warm[:, 0:1], func=ACT.Tanh)
 
         nc.sync.dma_start(offs_t[:], offs)
         nc.sync.dma_start(two_t[:], two)
@@ -62,13 +58,9 @@ def tile_picked_keypage_none_po_kernel(tc, x_words, x_scales, w1_words, w1_scale
         nc.sync.dma_start(out=ww[0][:].bitcast(I32), in_=w1_words[0].bitcast(I32))
         nc.sync.dma_start(out=xw[:], in_=x_words[0].rearrange("p n t -> p (n t)").bitcast(I32))
         load_scales(nc.sync, ws[0], w1_scales)
-        nc.sync.dma_start(slot_t[:], slot)
-        mem_rows = mem.rearrange("(p t) u -> t p u", t=PACK)
         nc.sync.dma_start(out=ww[1][:].bitcast(I32), in_=w2_words[0].bitcast(I32))
-        nc.sync.dma_start(out=page[0][:], in_=mem_rows[0])
         load_scales(nc.sync, ws[1], w2_scales)
-        for t in range(1, PACK):
-            nc.sync.dma_start(out=page[t][:], in_=mem_rows[t])
+        nc.sync.dma_start(slot_t[:], slot)
         nc.sync.dma_start(nq_t[:], nq)
         nc.gpsimd.dma_start(out=gb_t[:], in_=gb.rearrange("(p t) o -> p (t o)", t=PACK))
         nc.gpsimd.dma_start(out=ga_t[:], in_=ga.rearrange("(p t) o -> p (t o)", t=PACK))
@@ -79,11 +71,11 @@ def tile_picked_keypage_none_po_kernel(tc, x_words, x_scales, w1_words, w1_scale
         ga_signed = tile("ga_signed", [P, PACK], F32)
         nc.gpsimd.tensor_scalar(out=twice[:], in0=gb_t[:], scalar1=0.0, scalar2=2.0, op0=ALU.is_ge, op1=ALU.mult)
         nc.gpsimd.tensor_scalar(out=sign[:], in0=twice[:], scalar1=1.0, scalar2=-1.0, op0=ALU.mult, op1=ALU.add)
-        nc.gpsimd.tensor_tensor(out=gb_abs[:], in0=gb_t[:], in1=sign[:], op=ALU.mult)
+        nc.scalar.activation(out=gb_abs[:], in_=gb_t[:], func=ACT.Abs)
         nc.gpsimd.tensor_tensor(out=ga_signed[:], in0=ga_t[:], in1=sign[:], op=ALU.mult)
 
         lists = [offs_t, two_t]
-        pw = [tile("pw%d" % i, [P, S], U32) for i in range(2)]
+        pw = [tile("pw%d" % i, [P, S], U32, tag=["pw0", "ws0"][i]) for i in range(2)]
         pscale = [tile("pscale%d" % i, [P, S], U8) for i in range(2)]
         dw = [tile("dw%d" % i, [P, 2 * H], U8) for i in range(2)]
         ds = [tile("ds%d" % i, [P, H], U8) for i in range(2)]
@@ -122,6 +114,11 @@ def tile_picked_keypage_none_po_kernel(tc, x_words, x_scales, w1_words, w1_scale
         deal_words(1)
         deal_scales(1)
 
+        mem_rows = mem.rearrange("(p t) u -> t p u", t=PACK)
+        page = [tile("page%d" % t, [P, U], F32, tag=old) for t, old in enumerate(["xs", "ww0", "ww1", "xw"])]
+        for t in range(PACK):
+            nc.sync.dma_start(out=page[t][:], in_=mem_rows[t])
+
         a_sb = [tile("a_sb%d" % t, [P, S], F32) for t in range(PACK)]
         for t in range(PACK):
             bank = project(0, t)
@@ -138,72 +135,114 @@ def tile_picked_keypage_none_po_kernel(tc, x_words, x_scales, w1_words, w1_scale
             nc.vector.tensor_copy(page[t][:].indirect(slot_t[:]), a_sb[t][:])
             for g in range(GROUPS):
                 nc.scalar.activation(
-                    out=zb[g][:].rearrange("p (j m k) -> p j m k", j=PACK, k=PACK)[:, :, :, t],
-                    in_=page[t][:, 512 * g : 512 * (g + 1)].rearrange("p (m j) -> p j m", j=PACK),
+                    out=zb[g][:].rearrange("p (j c i k) -> p c j i k", j=PACK, i=2, k=PACK)[:, :, :, :, t],
+                    in_=page[t][:, 512 * g : 512 * (g + 1)].rearrange("p (c i j) -> p c j i", j=PACK, i=2),
                     func=ACT.Copy,
                     scale=ga_signed[:, t : t + 1],
                 )
 
-        zc = [tile("zc%d" % g, [P, 512], U32) for g in range(GROUPS)]
         zs = [tile("zs%d" % g, [P, 512], U8) for g in range(GROUPS)]
-        qc = [tile("qc%d" % h, [P, VH], U32) for h in range(HALVES)]
-        qs = [tile("qs%d" % h, [P, VH], U8) for h in range(HALVES)]
-        oc = [tile("oc%d" % g, [P, V], U32) for g in range(GROUPS)]
         osc = tile("osc", [P, GROUPS, V], U8)
+        chunks = [slice(0, 256), slice(256, 384), slice(384, 512)]
 
-        def queries(h):
-            got = tile("got%d" % h, [P, PACK, VH], F32, tag="got0" if h == 0 else "shared1")
-            for t in range(PACK):
-                nc.vector.tensor_copy(got[:, t, :], yw[t][:].indirect(nq_t[:, h * VH // 16 : (h + 1) * VH // 16]))
-            qb = tile("qb%d" % h, [P, PACK * VH], BF16)
+        def fetch(half, got, t):
+            nc.vector.tensor_copy(got[:, t, :], yw[t][:].indirect(nq_t[:, half * VH // 16 : (half + 1) * VH // 16]))
+
+        def larger(c, got, tag):
+            cols = chunks[c]
+            n = cols.stop - cols.start
+            qb = tile("qb%d" % c, [P, PACK * n], BF16, tag=tag)
             nc.vector.tensor_tensor(
                 out=qb[:].rearrange("p (c i t) -> p c t i", i=2, t=PACK),
-                in0=got[:].rearrange("p t (c i) -> p c t i", i=2),
-                in1=y_all[:, :, h * VH : (h + 1) * VH].rearrange("p t (c i) -> p c t i", i=2),
+                in0=got.rearrange("p t (c i) -> p c t i", i=2),
+                in1=y_all[:, :, cols].rearrange("p t (c i) -> p c t i", i=2),
                 op=ALU.max,
             )
-            nc.vector.quantize_mx(out=qc[h][:].bitcast(FP8X4), scales=qs[h][:], in_=qb[:])
+            return qb
 
-        def scores(h, g):
-            y = tile("y%d_%d" % (h, g), [P, PACK, VH], F32)
-            for pair in range(2):
-                bank = ps.tile([P, 2, VH], F32, name="score%d_%d_%d" % (h, g, pair), tag="bank%d" % (PACK * h + 2 * g + pair))
-                for e in range(2):
-                    j = 2 * pair + e
+        def queries(c, qb, tag):
+            n = chunks[c].stop - chunks[c].start
+            qc = tile("qc%d" % c, [P, n], U32, tag=tag)
+            qs = tile("qs%d" % c, [P, n], U8)
+            nc.vector.quantize_mx(out=qc[:].bitcast(FP8X4), scales=qs[:], in_=qb[:])
+            return qc, qs
+
+        def scores(c, g, query, first_bank):
+            cols = chunks[c]
+            n = cols.stop - cols.start
+            per_bank = 512 // n
+            y = tile("y%d_%d" % (c, g), [P, PACK, n], F32)
+            for b in range(PACK // per_bank):
+                bank = ps.tile([P, per_bank, n], F32, name="score%d_%d_%d" % (c, g, b), tag="bank%d" % (first_bank + b))
+                for e in range(per_bank):
+                    j = per_bank * b + e
                     nc.tensor.matmul_mx(
                         out=bank[:, e, :],
                         lhsT=zc[g][:, P * j : P * (j + 1)].bitcast(FP8X4),
                         lhsT_scale=zs[g][:, P * j : P * (j + 1)],
-                        rhs=qc[h][:].bitcast(FP8X4),
-                        rhs_scale=qs[h][:],
+                        rhs=query[0][:].bitcast(FP8X4),
+                        rhs_scale=query[1][:],
                         start=True,
                         stop=True,
                     )
-                nc.scalar.activation(out=y[:, 2 * pair : 2 * pair + 2, :], in_=bank[:], func=ACT.Tanh, scale=0.0625)
-            cols = slice(h * VH, (h + 1) * VH)
+                nc.scalar.activation(out=y[:, per_bank * b : per_bank * (b + 1), :], in_=bank[:], func=ACT.Tanh, scale=0.0625)
             nc.sync.dma_start(out=out_0[512 * g : 512 * (g + 1), cols].rearrange("(p j) v -> p j v", j=PACK), in_=y[:])
             return y
 
-        def planes(h, g, y):
-            yb = tile("yb%d_%d" % (h, g), [P, PACK * VH], BF16)
-            nc.vector.tensor_copy(
-                out=yb[:].rearrange("p (c i j) -> p c j i", i=2, j=PACK),
-                in_=y[:].rearrange("p j (c i) -> p c j i", i=2),
-            )
-            cols = slice(h * VH, (h + 1) * VH)
+        def weave(c, g, y, copy, tag):
+            n = chunks[c].stop - chunks[c].start
+            yb = tile("yb%d_%d" % (c, g), [P, PACK * n], BF16, tag=tag)
+            copy(out=yb[:].rearrange("p (c i j) -> p c j i", i=2, j=PACK), in_=y[:].rearrange("p j (c i) -> p c j i", i=2))
+            return yb
+
+        def weave_on_scalar(c, g, y):
+            n = chunks[c].stop - chunks[c].start
+            yb = tile("yb%d_%d" % (c, g), [P, PACK * n], BF16)
+            nc.scalar.copy(out=yb[:].rearrange("p (v j) -> p v j", j=PACK), in_=y[:].rearrange("p j v -> p v j"))
+            return yb
+
+        def planes(c, g, yb):
+            cols = chunks[c]
             nc.vector.quantize_mx(out=oc[g][:, cols].bitcast(FP8X4), scales=osc[:, g, cols], in_=yb[:])
+
+        def store_words(g, cols):
             nc.sync.dma_start(out=out_1[g].rearrange("p v t -> p (v t)").bitcast(I32)[:, cols], in_=oc[g][:, cols].bitcast(I32))
 
-        queries(0)
+        got0 = tile("got0", [P, PACK, VH], F32, tag="a_sb3")
+        for t in range(PACK):
+            fetch(0, got0, t)
+        zc = [tile("zc0", [P, 512], U32)]
+        nc.vector.quantize_mx(out=zc[0][:].bitcast(FP8X4), scales=zs[0][:], in_=zb[0][:])
+        qb0 = larger(0, got0[:], "shared0")
+        q0 = queries(0, qb0, None)
+        zc.append(tile("zc1", [P, 512], U32, tag="shared0"))
+        nc.vector.quantize_mx(out=zc[1][:].bitcast(FP8X4), scales=zs[1][:], in_=zb[1][:])
+        got1 = tile("got1", [P, PACK, VH], F32, tag="shared1")
+        for t in range(PACK):
+            fetch(1, got1, t)
+        y0 = [scores(0, g, q0, 2 * g) for g in range(GROUPS)]
+        yb00 = weave_on_scalar(0, 0, y0[0])
+        qb1 = larger(1, got1[:, :, 0:128], None)
+        qb2 = larger(2, got1[:, :, 128:256], None)
+        q1 = queries(1, qb1, None)
+        q2 = queries(2, qb2, None)
+        y1 = [scores(1, g, q1, 4 + g) for g in range(GROUPS)]
+        y2 = [scores(2, g, q2, 6 + g) for g in range(GROUPS)]
+        oc = [tile("oc0", [P, V], U32, tag="qb1"), tile("oc1", [P, V], U32)]
+        yb01 = weave(0, 1, y0[1], nc.vector.tensor_copy, "qb2")
+        planes(0, 0, yb00)
+        store_words(0, chunks[0])
+        yb1 = [weave(1, 0, y1[0], nc.vector.tensor_copy, None)]
+        planes(0, 1, yb01)
+        store_words(1, chunks[0])
+        yb1.append(weave(1, 1, y1[1], nc.vector.tensor_copy, None))
+        planes(1, 0, yb1[0])
+        yb2 = [weave(2, 0, y2[0], nc.vector.tensor_copy, None)]
+        planes(1, 1, yb1[1])
+        yb2.append(weave(2, 1, y2[1], nc.vector.tensor_copy, None))
         for g in range(GROUPS):
-            nc.vector.quantize_mx(out=zc[g][:].bitcast(FP8X4), scales=zs[g][:], in_=zb[g][:])
-        first = [scores(0, g) for g in range(GROUPS)]
-        queries(1)
-        second = [scores(1, g) for g in range(GROUPS)]
-        for g in range(GROUPS):
-            planes(0, g, first[g])
-        for g in range(GROUPS):
-            planes(1, g, second[g])
+            planes(2, g, yb2[g])
+            store_words(g, slice(256, 512))
         for q in range(4):
             queue = nc.sync if q % 2 == 0 else nc.scalar
             queue.dma_start(

from contextlib import ExitStack

import concourse.mybir as mybir

F32 = mybir.dt.float32
BF16 = mybir.dt.bfloat16
I32 = mybir.dt.int32
U32 = mybir.dt.uint32
U16 = mybir.dt.uint16
U8 = mybir.dt.uint8
FP8X4 = mybir.dt.float8_e4m3fn_x4
FP4X4 = mybir.dt.float4_e2m1fn_x4
ALU = mybir.AluOpType
ACT = mybir.ActivationFunctionType

K, T, S, V, H, U = 512, 2048, 512, 512, 512, 1024
P = 128
PACK = 4
GROUPS = U // 512
HALVES = 2
VH = V // HALVES

FLOPS = 2 * K * H * S + 2 * K * H * V + 2 * H * U * V


def tile_picked_keypage_none_po_kernel(tc, x_words, x_scales, w1_words, w1_scales, w2_words, w2_scales, mem, ga, gb, offs, two, slot, nq, out_0, out_1, out_2):
    nc = tc.nc
    with ExitStack() as ctx:
        sb = ctx.enter_context(tc.tile_pool(name="sb", bufs=1))
        ps = ctx.enter_context(tc.psum_pool(name="ps", bufs=1))

        def tile(name, shape, dtype, tag=None):
            return sb.tile(shape, dtype, name=name, tag=tag or name, align_bytes=64)

        offs_t = sb.tile([P, S // 16], U16, name="offs_t")
        two_t = sb.tile([P, V // 16], U16, name="two_t")
        slot_t = sb.tile([P, S // 16], U16, name="slot_t")
        nq_t = sb.tile([P, V // 16], U16, name="nq_t")

        xw = tile("xw", [P, T], I32)
        xs = tile("xs", [P, T], U8)
        ww = [tile("ww%d" % i, [P, 2 * H], U8) for i in range(2)]
        ws = [tile("ws%d" % i, [P, H], U8) for i in range(2)]
        ga_t = tile("ga_t", [P, PACK], F32)
        gb_t = tile("gb_t", [P, PACK], F32)

        def load_scales(queue, dst, src):
            for q in range(4):
                queue.dma_start(out=dst[32 * q : 32 * q + 4, :].bitcast(I32), in_=src[0, 4 * q : 4 * q + 4, :].bitcast(I32))

        nc.gpsimd.memset(xs[:].bitcast(I32), 0)
        nc.vector.memset(ws[0][:].bitcast(I32), 0)
        nc.vector.memset(ws[1][:].bitcast(I32), 0)

        nc.sync.dma_start(offs_t[:], offs)
        nc.sync.dma_start(two_t[:], two)
        load_scales(nc.sync, xs, x_scales)
        nc.sync.dma_start(out=ww[0][:].bitcast(I32), in_=w1_words[0].bitcast(I32))
        nc.sync.dma_start(out=xw[:], in_=x_words[0].rearrange("p n t -> p (n t)").bitcast(I32))
        load_scales(nc.sync, ws[0], w1_scales)
        nc.sync.dma_start(out=ww[1][:].bitcast(I32), in_=w2_words[0].bitcast(I32))
        load_scales(nc.sync, ws[1], w2_scales)
        nc.sync.dma_start(slot_t[:], slot)
        nc.sync.dma_start(nq_t[:], nq)
        nc.gpsimd.dma_start(out=gb_t[:], in_=gb.rearrange("(p t) o -> p (t o)", t=PACK))
        nc.gpsimd.dma_start(out=ga_t[:], in_=ga.rearrange("(p t) o -> p (t o)", t=PACK))

        twice = tile("twice", [P, PACK], F32)
        sign = tile("sign", [P, PACK], F32)
        gb_abs = tile("gb_abs", [P, PACK], F32)
        ga_signed = tile("ga_signed", [P, PACK], F32)
        nc.gpsimd.tensor_scalar(out=twice[:], in0=gb_t[:], scalar1=0.0, scalar2=2.0, op0=ALU.is_ge, op1=ALU.mult)
        nc.gpsimd.tensor_scalar(out=sign[:], in0=twice[:], scalar1=1.0, scalar2=-1.0, op0=ALU.mult, op1=ALU.add)
        nc.scalar.activation(out=gb_abs[:], in_=gb_t[:], func=ACT.Abs)
        nc.gpsimd.tensor_tensor(out=ga_signed[:], in0=ga_t[:], in1=sign[:], op=ALU.mult)

        lists = [offs_t, two_t]
        pw = [tile("pw%d" % i, [P, S], U32, tag=["pw0", "ws0"][i]) for i in range(2)]
        pscale = [tile("pscale%d" % i, [P, S], U8) for i in range(2)]
        dw = [tile("dw%d" % i, [P, 2 * H], U8) for i in range(2)]
        ds = [tile("ds%d" % i, [P, H], U8) for i in range(2)]

        def gather_scales(i):
            nc.vector.tensor_copy(pscale[i][:], xs[:].indirect(lists[i][:]))

        def gather_words(i):
            nc.vector.tensor_copy(pw[i][:], xw[:].bitcast(U32).indirect(lists[i][:]))

        def deal_words(i):
            nc.vector.tensor_copy(out=dw[i][:].rearrange("p (t m b) -> p t m b", t=PACK, b=2), in_=ww[i][:].rearrange("p (m t b) -> p t m b", t=PACK, b=2))

        def deal_scales(i):
            nc.vector.tensor_copy(out=ds[i][:].rearrange("p (t m) -> p t m", t=PACK), in_=ws[i][:].rearrange("p (m t) -> p t m", t=PACK))

        def project(i, t):
            bank = ps.tile([P, S], F32, name="proj%d_%d" % (i, t), tag="bank%d" % (PACK * i + t))
            nc.tensor.matmul_mx(
                out=bank[:],
                lhsT=dw[i][:, 2 * P * t : 2 * P * (t + 1)].bitcast(FP4X4),
                lhsT_scale=ds[i][:, P * t : P * (t + 1)],
                rhs=pw[i][:].bitcast(FP8X4),
                rhs_scale=pscale[i][:],
                start=True,
                stop=True,
            )
            return bank

        gather_scales(0)
        gather_scales(1)
        deal_words(0)
        gather_words(0)
        deal_scales(0)
        gather_words(1)
        deal_words(1)
        deal_scales(1)

        mem_rows = mem.rearrange("(p t) u -> t p u", t=PACK)
        page = [tile("page%d" % t, [P, U], F32, tag=old) for t, old in enumerate(["xs", "ww0", "ww1", "xw"])]
        for t in range(PACK):
            nc.sync.dma_start(out=page[t][:], in_=mem_rows[t])

        a_sb = [tile("a_sb%d" % t, [P, S], F32) for t in range(PACK)]
        for t in range(PACK):
            bank = project(0, t)
            nc.scalar.copy(out=a_sb[t][:], in_=bank[:])
        yw = [tile("yw%d" % t, [P, V], F32) for t in range(PACK)]
        y_all = tile("y_all", [P, PACK, V], F32)
        for t in range(PACK):
            bank = project(1, t)
            nc.scalar.activation(out=yw[t][:], in_=bank[:], func=ACT.Copy, scale=gb_abs[:, t : t + 1])
            nc.sync.dma_start(out=y_all[:, t, :], in_=yw[t][:])

        zb = [tile("zb%d" % g, [P, PACK * 512], BF16, tag="shared%d" % g) for g in range(GROUPS)]
        for t in range(PACK):
            nc.vector.tensor_copy(page[t][:].indirect(slot_t[:]), a_sb[t][:])
            for g in range(GROUPS):
                nc.scalar.activation(
                    out=zb[g][:].rearrange("p (j c i k) -> p c j i k", j=PACK, i=2, k=PACK)[:, :, :, :, t],
                    in_=page[t][:, 512 * g : 512 * (g + 1)].rearrange("p (c i j) -> p c j i", j=PACK, i=2),
                    func=ACT.Copy,
                    scale=ga_signed[:, t : t + 1],
                )

        zs = [tile("zs%d" % g, [P, 512], U8) for g in range(GROUPS)]
        osc = tile("osc", [P, GROUPS, V], U8)
        chunks = [slice(0, 256), slice(256, 384), slice(384, 512)]

        def fetch(half, got, t):
            nc.vector.tensor_copy(got[:, t, :], yw[t][:].indirect(nq_t[:, half * VH // 16 : (half + 1) * VH // 16]))

        def larger(c, got, tag):
            cols = chunks[c]
            n = cols.stop - cols.start
            qb = tile("qb%d" % c, [P, PACK * n], BF16, tag=tag)
            nc.vector.tensor_tensor(
                out=qb[:].rearrange("p (c i t) -> p c t i", i=2, t=PACK),
                in0=got.rearrange("p t (c i) -> p c t i", i=2),
                in1=y_all[:, :, cols].rearrange("p t (c i) -> p c t i", i=2),
                op=ALU.max,
            )
            return qb

        def queries(c, qb, tag):
            n = chunks[c].stop - chunks[c].start
            qc = tile("qc%d" % c, [P, n], U32, tag=tag)
            qs = tile("qs%d" % c, [P, n], U8)
            nc.vector.quantize_mx(out=qc[:].bitcast(FP8X4), scales=qs[:], in_=qb[:])
            return qc, qs

        def scores(c, g, query, first_bank):
            cols = chunks[c]
            n = cols.stop - cols.start
            per_bank = 512 // n
            y = tile("y%d_%d" % (c, g), [P, PACK, n], F32)
            for b in range(PACK // per_bank):
                bank = ps.tile([P, per_bank, n], F32, name="score%d_%d_%d" % (c, g, b), tag="bank%d" % (first_bank + b))
                for e in range(per_bank):
                    j = per_bank * b + e
                    nc.tensor.matmul_mx(
                        out=bank[:, e, :],
                        lhsT=zc[g][:, P * j : P * (j + 1)].bitcast(FP8X4),
                        lhsT_scale=zs[g][:, P * j : P * (j + 1)],
                        rhs=query[0][:].bitcast(FP8X4),
                        rhs_scale=query[1][:],
                        start=True,
                        stop=True,
                    )
                nc.scalar.activation(out=y[:, per_bank * b : per_bank * (b + 1), :], in_=bank[:], func=ACT.Tanh, scale=0.0625)
            nc.sync.dma_start(out=out_0[512 * g : 512 * (g + 1), cols].rearrange("(p j) v -> p j v", j=PACK), in_=y[:])
            return y

        def weave(c, g, y, copy, tag):
            n = chunks[c].stop - chunks[c].start
            yb = tile("yb%d_%d" % (c, g), [P, PACK * n], BF16, tag=tag)
            copy(out=yb[:].rearrange("p (c i j) -> p c j i", i=2, j=PACK), in_=y[:].rearrange("p j (c i) -> p c j i", i=2))
            return yb

        def weave_on_scalar(c, g, y):
            n = chunks[c].stop - chunks[c].start
            yb = tile("yb%d_%d" % (c, g), [P, PACK * n], BF16)
            nc.scalar.copy(out=yb[:].rearrange("p (v j) -> p v j", j=PACK), in_=y[:].rearrange("p j v -> p v j"))
            return yb

        def planes(c, g, yb):
            cols = chunks[c]
            nc.vector.quantize_mx(out=oc[g][:, cols].bitcast(FP8X4), scales=osc[:, g, cols], in_=yb[:])

        def store_words(g, cols):
            nc.sync.dma_start(out=out_1[g].rearrange("p v t -> p (v t)").bitcast(I32)[:, cols], in_=oc[g][:, cols].bitcast(I32))

        got0 = tile("got0", [P, PACK, VH], F32, tag="a_sb3")
        for t in range(PACK):
            fetch(0, got0, t)
        zc = [tile("zc0", [P, 512], U32)]
        nc.vector.quantize_mx(out=zc[0][:].bitcast(FP8X4), scales=zs[0][:], in_=zb[0][:])
        qb0 = larger(0, got0[:], "shared0")
        q0 = queries(0, qb0, None)
        zc.append(tile("zc1", [P, 512], U32, tag="shared0"))
        nc.vector.quantize_mx(out=zc[1][:].bitcast(FP8X4), scales=zs[1][:], in_=zb[1][:])
        got1 = tile("got1", [P, PACK, VH], F32, tag="shared1")
        for t in range(PACK):
            fetch(1, got1, t)
        y0 = [scores(0, g, q0, 2 * g) for g in range(GROUPS)]
        yb00 = weave_on_scalar(0, 0, y0[0])
        qb1 = larger(1, got1[:, :, 0:128], None)
        qb2 = larger(2, got1[:, :, 128:256], None)
        q1 = queries(1, qb1, None)
        q2 = queries(2, qb2, None)
        y1 = [scores(1, g, q1, 4 + g) for g in range(GROUPS)]
        y2 = [scores(2, g, q2, 6 + g) for g in range(GROUPS)]
        oc = [tile("oc0", [P, V], U32, tag="qb1"), tile("oc1", [P, V], U32)]
        yb01 = weave(0, 1, y0[1], nc.vector.tensor_copy, "qb2")
        planes(0, 0, yb00)
        store_words(0, chunks[0])
        yb1 = [weave(1, 0, y1[0], nc.vector.tensor_copy, None)]
        planes(0, 1, yb01)
        store_words(1, chunks[0])
        yb1.append(weave(1, 1, y1[1], nc.vector.tensor_copy, None))
        planes(1, 0, yb1[0])
        yb2 = [weave(2, 0, y2[0], nc.vector.tensor_copy, None)]
        planes(1, 1, yb1[1])
        yb2.append(weave(2, 1, y2[1], nc.vector.tensor_copy, None))
        for g in range(GROUPS):
            planes(2, g, yb2[g])
            store_words(g, slice(256, 512))
        for q in range(4):
            queue = nc.sync if q % 2 == 0 else nc.scalar
            queue.dma_start(
                out=out_2[:, 4 * q : 4 * q + 4, :].rearrange("g r v -> r g v").bitcast(I32),
                in_=osc[32 * q : 32 * q + 4, :, :].bitcast(I32),
            )
